import numpy as np
import ml_dtypes


def mxq(x, axis, fmt="e4m3"):
    dtype, down = {"e4m3": (ml_dtypes.float8_e4m3fn, 7), "e5m2": (ml_dtypes.float8_e5m2, 14)}[fmt]
    v = np.moveaxis(np.asarray(x, np.float32).astype(ml_dtypes.bfloat16).astype(np.float64), axis, -1)
    blocks = v.reshape(v.shape[:-1] + (-1, 32))
    amax = np.abs(blocks).max(-1, keepdims=True)
    byte = np.maximum(np.where(amax > 0, np.frexp(amax)[1] - 1 + 127, 0) - down, 1)
    scale = np.exp2(byte - 127.0)
    codes = (blocks / scale).astype(np.float32).astype(dtype).astype(np.float64)
    return np.moveaxis((codes * scale).reshape(v.shape), -1, axis)


WIDE = False


def mx_kscale(k):
    if not WIDE:
        return np.ones(k)
    levels = np.array([10, -10, 5, -5, 0])
    if k % 512:
        return np.exp2(np.random.permutation(np.resize(levels, k // 32))).repeat(32)
    a = np.empty((k // 512, 16))
    for p in range(k // 512):
        a[p, :8] = np.random.permutation(np.resize(levels, 8))
        for g in range(8):
            far = levels[np.abs(levels - a[p, g]) >= 10]
            a[p, g + 8] = far[np.random.randint(len(far))]
    return np.exp2(a.ravel()).repeat(32)


def f64(x):
    return np.asarray(x).astype(np.float64)


def striped(idx):
    return np.tile(idx.reshape(-1, 16).T, (8, 1)).astype(np.uint16)


def unstriped(offs):
    return offs[:16].T.reshape(-1).astype(np.int64)


E2M1 = np.array([0.0, 0.5, 1.0, 1.5, 2.0, 3.0, 4.0, 6.0, -0.0, -0.5, -1.0, -1.5, -2.0, -3.0, -4.0, -6.0])


def pack_weight(w, fmt):
    k, n = w.shape
    w = f64(np.asarray(w, np.float32).astype(ml_dtypes.bfloat16)).reshape(k // 32, 32, n)
    amax = np.abs(w).max(1)
    if fmt == "e4m3":
        byte = np.frexp(amax)[1] - 1 + 127 - 7
    else:
        mant, ex = np.frexp(amax / 6.0)
        byte = np.where(mant > 0.5, ex, ex - 1) + 127
    byte = np.clip(np.where(amax > 0, byte, 1), 1, 254)
    scaled = (w * np.exp2(127.0 - byte)[:, None, :]).reshape(k, n).astype(np.float32)
    by_word = np.ascontiguousarray(scaled.reshape(k // 512, 128, 4, n).transpose(0, 1, 3, 2))
    if fmt == "e4m3":
        words = by_word.astype(ml_dtypes.float8_e4m3fn).view(np.uint8)
    else:
        c = by_word.astype(ml_dtypes.float4_e2m1fn).view(np.uint8) & 0xF
        words = (c[..., 0::2] | (c[..., 1::2] << 4)).reshape(k // 512, 128, 2 * n)
    return np.ascontiguousarray(words), np.ascontiguousarray(byte.astype(np.uint8).reshape(k // 512, 16, n))


def unpack_weight(words, scales, fmt):
    g, _, n = scales.shape
    words = np.ascontiguousarray(words).reshape(g, 128, n, -1)
    if fmt == "e4m3":
        vals = words.view(ml_dtypes.float8_e4m3fn).astype(np.float64)
    else:
        nib = np.empty((g, 128, n, 4), np.uint8)
        nib[..., 0::2] = words & 0xF
        nib[..., 1::2] = words >> 4
        vals = E2M1[nib]
    vals = vals * np.repeat(np.exp2(scales.astype(np.float64) - 127.0), 8, axis=1)[..., None]
    return vals.transpose(0, 1, 3, 2).reshape(g * 512, n)


def gelu(v):
    return 0.5 * v * (1.0 + np.tanh(np.sqrt(2.0 / np.pi) * (v + 0.044715 * v**3)))


def striped8(idx):
    return np.concatenate([v.reshape(-1, 16).T for v in idx]).astype(np.uint16)


def unstriped8(offs):
    return np.stack([offs[16 * g:16 * g + 16].T.reshape(-1) for g in range(8)]).astype(np.int64)


def heads(h, wgt, idx8):
    r = np.arange(h.shape[0])
    return wgt[r // 4 % 128] * h[r[:, None], idx8[r % 512 // 64]]


def put_heads(h, wgs, idx8, t2):
    r = np.arange(h.shape[0])
    page = np.zeros((h.shape[0], t2))
    page[r[:, None], idx8[r % 512 // 64]] = wgs[r // 4 % 128] * h
    return page


T, S, P, T2, K, H = 4096, 1024, 512, 1024, 1536, 1024

def setup_inputs():
    n = np.random.standard_normal
    s = mx_kscale(K)[:, None]
    u = mx_kscale(H)[:, None]
    d = {}
    d["tab_words"], d["tab_scales"] = pack_weight(n((K, T)) * s, "e4m3")
    d["offs"] = striped(np.random.permutation(T)[:S])
    d["w1"] = (n((K, H)) / K ** 0.5 / s * u.T).astype(np.float32)
    d["b1"] = (0.5 * n(H) * u[:, 0]).astype(np.float32)
    d["offs2"] = striped8(np.stack([np.random.permutation(S)[:P] for _ in range(8)]))
    d["wgt"] = np.repeat(np.random.uniform(0.5, 2.0, (8, P)), 16, axis=0).astype(np.float32)
    d["base"] = (0.5 * n(H) * u[:, 0]).astype(np.float32)
    d["w4_words"], d["w4_scales"] = pack_weight(n((H, H)) / H ** 0.5 / u, "e2m1")
    d["foam"] = (n((H, P)) * u).astype(np.float32)
    d["wf_words"], d["wf_scales"] = pack_weight(1.5 * n((H, H)) / H ** 0.5 / u, "e4m3")
    d["rho"] = (0.6 * n(H) / u[:, 0]).astype(np.float32)
    d["offs3"] = striped8(np.stack([np.random.permutation(T2)[:P] for _ in range(8)]))
    d["wgo"] = np.repeat(np.random.uniform(0.5, 2.0, (8, P)), 16, axis=0).astype(np.float32)
    return d

def reference(tab_words, tab_scales, offs, w1, b1, offs2, wgt, base, w4_words, w4_scales,
              foam, wf_words, wf_scales, rho, offs3, wgo):
    v = unpack_weight(tab_words, tab_scales, "e4m3")[:, unstriped(offs)]
    h = (mxq(f64(w1), 0, "e4m3").T @ v) + f64(b1)[:, None]
    x = heads(h, f64(wgt), unstriped8(offs2))
    z = np.maximum(x, f64(base)[:, None])
    w4 = unpack_weight(w4_words, w4_scales, "e2m1")
    comfort = w4.T @ mxq(z, 0, "e4m3")
    wf = unpack_weight(wf_words, wf_scales, "e4m3")
    resp = wf.T @ mxq(f64(foam), 0, "e4m3")
    y = comfort / (1.0 + np.abs(resp)) + f64(rho)[:, None] * x
    return put_heads(y, f64(wgo), unstriped8(offs3), T2)

@@ -1,0 +1,327 @@
+from contextlib import ExitStack
+
+import concourse.mybir as mybir
+from concourse.masks import make_identity
+
+T, S, M, T2, K, H = 4096, 1024, 512, 1024, 1536, 1024
+FLOPS = 2 * (K * H * S + 2 * H * H * M)
+
+F32 = mybir.dt.float32
+BF16 = mybir.dt.bfloat16
+I32 = mybir.dt.int32
+U32 = mybir.dt.uint32
+U16 = mybir.dt.uint16
+U8 = mybir.dt.uint8
+FP8X4 = mybir.dt.float8_e4m3fn_x4
+FP4X4 = mybir.dt.float4_e2m1fn_x4
+ALU = mybir.AluOpType
+ACT = mybir.ActivationFunctionType
+
+P = 128
+PACK = 4
+BLOCK = P * PACK
+PASSES = K // BLOCK
+BLOCKS = H // BLOCK
+BANK = 512
+HALF = 256
+
+
+def tile_list_mattress_comfort_filing_kernel(
+    tc, tab_words, tab_scales, offs, w1, b1, offs2, wgt, base, w4_words, w4_scales,
+    foam, wf_words, wf_scales, rho, offs3, wgo, out,
+):
+    nc = tc.nc
+    with ExitStack() as ctx:
+        keep = ctx.enter_context(tc.tile_pool(name="keep", bufs=1))
+        ring = ctx.enter_context(tc.tile_pool(name="ring", bufs=1))
+        psum = ctx.enter_context(tc.psum_pool(name="psum", bufs=1))
+
+        def bank(k):
+            return psum.tile([P, BANK], F32, name="bank%d" % k)
+
+        offs_sb = keep.tile([P, S // 16], U16, name="offs_sb")
+        offs2_sb = keep.tile([P, M // 16], U16, name="offs2_sb")
+        offs3_sb = keep.tile([P, M // 16], U16, name="offs3_sb")
+        tab_planes = keep.tile([P, T], U8, name="tab_planes", align_bytes=64)
+        w_planes = keep.tile([P, BLOCKS, H], U8, name="w_planes", align_bytes=64)
+        one = keep.tile([P, 1], F32, name="one")
+        warm = keep.tile([P, 1], F32, name="warm")
+        ident = keep.tile([P, P], F32, name="ident")
+        nc.vector.memset(tab_planes[:].bitcast(I32), 0)
+        nc.vector.memset(w_planes[:].bitcast(I32), 0)
+        nc.vector.memset(one[:], 1.0)
+        nc.scalar.activation(warm[:], one[:], ACT.Abs_reciprocal_sqrt, bias=one[:])
+
+        def load_vector(vec, name):
+            sb = keep.tile([P, BLOCKS, PACK], F32, name=name)
+            nc.gpsimd.dma_start(out=sb[:], in_=vec.rearrange("(b p i) -> p b i", b=BLOCKS, i=PACK))
+            return sb
+
+        b1_sb = load_vector(b1, "b1_sb")
+        base_sb = load_vector(base, "base_sb")
+        rho_sb = load_vector(rho, "rho_sb")
+        for first, scales in ((4, wf_scales), (0, w4_scales)):
+            for q in range(4):
+                nc.gpsimd.dma_start(
+                    out=w_planes[32 * q + first : 32 * q + first + 4, :, :].bitcast(I32),
+                    in_=scales[:, 4 * q : 4 * q + 4, :].bitcast(I32).rearrange("a r n -> r a n"),
+                )
+        make_identity(nc, ident[:])
+
+        def load_rows(rows):
+            raw = ring.tile([P, PACK, BLOCK], F32, name="raw", bufs=5)
+            nc.sync.dma_start(out=raw[:], in_=rows.rearrange("(p j) c -> p j c", j=PACK))
+            return raw
+
+        def load_w1(b, a):
+            return load_rows(w1[a * BLOCK : (a + 1) * BLOCK, b * BLOCK : (b + 1) * BLOCK])
+
+        def load_table(a):
+            words = keep.tile([P, T], I32, name="tab%d" % a, align_bytes=64)
+            nc.sync.dma_start(out=words[:], in_=tab_words[a].rearrange("p t i -> p (t i)").bitcast(I32))
+            return words
+
+        w1_raw = {}
+        table = {}
+        table[0] = load_table(0)
+        for q in range(4):
+            nc.sync.dma_start(
+                out=tab_planes[32 * q : 32 * q + 4 * PASSES, :].bitcast(I32),
+                in_=tab_scales[:, 4 * q : 4 * q + 4, :].bitcast(I32),
+            )
+        nc.sync.dma_start(offs_sb[:], offs)
+        w1_raw[0, 0] = load_w1(0, 0)
+        w1_raw[0, 1] = load_w1(0, 1)
+        table[1] = load_table(1)
+        nc.sync.dma_start(offs2_sb[:], offs2)
+        wgt_sb = keep.tile([P, M], F32, name="wgt_sb")
+        nc.sync.dma_start(out=wgt_sb[:], in_=wgt)
+        table[2] = load_table(2)
+        w1_raw[0, 2] = load_w1(0, 2)
+        for a in range(PASSES):
+            w1_raw[1, a] = load_w1(1, a)
+
+        pages = [keep.tile([P, T2], F32, name="page%d" % i) for i in range(PACK)]
+        for page in pages:
+            nc.vector.memset(page[:], 0.0)
+
+        def copy_on(engine, dst, src):
+            if engine == "vector":
+                nc.vector.tensor_copy(out=dst, in_=src)
+            else:
+                nc.scalar.copy(out=dst, in_=src)
+
+        def quantise(grouped, name):
+            codes = keep.tile([P, HALF], U32, name=name + "_codes", align_bytes=64)
+            scales = keep.tile([P, HALF], U8, name=name + "_scales", align_bytes=64)
+            nc.vector.quantize_mx(out=codes[:].bitcast(FP8X4), scales=scales[:], in_=grouped[:])
+            return codes, scales
+
+        def new_grouped():
+            return ring.tile([P, HALF * PACK], BF16, name="grouped", bufs=4, align_bytes=64)
+
+        def round_w1(b, a, u, engine):
+            grouped = new_grouped()
+            src = w1_raw[b, a][:].rearrange("p j (m i) -> p m j i", i=PACK)[:, :, :, 2 * u : 2 * u + 2]
+            copy_on(engine, grouped[:].rearrange("p (i m j) -> p m j i", i=2, j=PACK), src)
+            return grouped
+
+        w1_q = {}
+
+        def prepare_w1(b, a, engines):
+            grouped = [round_w1(b, a, u, engines[u]) for u in range(2)]
+            for u in range(2):
+                w1_q[b, a, u] = quantise(grouped[u], "w1_%d%d%d" % (b, a, u))
+
+        picked = {}
+
+        def pick_words(a):
+            picked[a] = keep.tile([P, S], U32, name="picked%d" % a, align_bytes=64)
+            nc.vector.tensor_copy(out=picked[a][:], in_=table[a][:].bitcast(U32).indirect(offs_sb[:]))
+
+        picked_planes = keep.tile([P, S], U8, name="picked_planes", align_bytes=64)
+
+        def first_pass(b, a, banks, i):
+            codes, scales = w1_q[b, a, i // 2]
+            cols = slice((i % 2) * P, (i % 2 + 1) * P)
+            for half in range(2):
+                toks = slice(half * BANK, (half + 1) * BANK)
+                nc.tensor.matmul_mx(
+                    out=banks[2 * i + half][:],
+                    lhsT=codes[:, cols].bitcast(FP8X4),
+                    lhsT_scale=scales[:, cols],
+                    rhs=picked[a][:, toks].bitcast(FP8X4),
+                    rhs_scale=picked_planes[4 * a : P, toks],
+                    start=(a == 0),
+                    stop=(a == PASSES - 1),
+                )
+
+        x = [keep.tile([P, PACK, M], F32, name="x%d" % b) for b in range(BLOCKS)]
+
+        def make_h(b, banks, i):
+            h = ring.tile([P, S], F32, name="h", bufs=4)
+            for half in range(2):
+                nc.scalar.activation(
+                    h[:, half * BANK : (half + 1) * BANK], banks[2 * i + half][:], ACT.Identity,
+                    bias=b1_sb[:, b, i : i + 1],
+                )
+            return h
+
+        def pick_x(b, i, h):
+            nc.vector.tensor_tensor(x[b][:, i, :], h[:].indirect(offs2_sb[:]), wgt_sb[:], ALU.mult)
+
+        def round_z(b, half):
+            grouped = new_grouped()
+            src = x[b][:, :, half * HALF : (half + 1) * HALF].rearrange("p i (c e) -> p c i e", e=4)
+            floor = base_sb[:, b, :].unsqueeze(1).unsqueeze(3).to_broadcast([P, HALF // 4, PACK, 4])
+            nc.vector.tensor_tensor(
+                grouped[:].rearrange("p (c e i) -> p c i e", e=4, i=PACK), src, floor, ALU.max
+            )
+            return grouped
+
+        z_q = {}
+
+        def prepare_z(b):
+            grouped = [round_z(b, half) for half in range(2)]
+            for half in range(2):
+                z_q[b, half] = quantise(grouped[half], "z_%d%d" % (b, half))
+
+        pick_words(0)
+        nc.vector.tensor_copy(out=picked_planes[:], in_=tab_planes[:].indirect(offs_sb[:]))
+        prepare_w1(0, 0, ("scalar", "scalar"))
+        banks = [bank(k) for k in range(8)]
+        for i in range(PACK):
+            first_pass(0, 0, banks, i)
+        prepare_w1(0, 1, ("scalar", "scalar"))
+        pick_words(1)
+        for i in range(PACK):
+            first_pass(0, 1, banks, i)
+        pick_words(2)
+        prepare_w1(0, 2, ("vector", "scalar"))
+        h0 = []
+        for i in range(PACK):
+            first_pass(0, 2, banks, i)
+            h0.append(make_h(0, banks, i))
+
+        foam_raw = [load_rows(foam[b * BLOCK : (b + 1) * BLOCK, :]) for b in range(BLOCKS)]
+        wf_sb = keep.tile([P, BLOCKS, H], I32, name="wf_sb", align_bytes=64)
+        nc.sync.dma_start(out=wf_sb[:], in_=wf_words.rearrange("a p c i -> p a (c i)").bitcast(I32))
+        w4_sb = keep.tile([P, BLOCKS, 2 * H], U8, name="w4_sb", align_bytes=64)
+        nc.sync.dma_start(out=w4_sb[:].bitcast(I32), in_=w4_words.rearrange("a p c -> p a c").bitcast(I32))
+        nc.sync.dma_start(offs3_sb[:], offs3)
+        wgo_sb = keep.tile([P, M], F32, name="wgo_sb")
+        nc.sync.dma_start(out=wgo_sb[:], in_=wgo)
+
+        banks = [bank(k) for k in range(8)]
+        prepare_w1(1, 0, ("vector", "vector"))
+        pick_x(0, 0, h0[0])
+        pick_x(0, 1, h0[1])
+        for i in range(PACK):
+            first_pass(1, 0, banks, i)
+        prepare_w1(1, 1, ("scalar", "scalar"))
+        pick_x(0, 2, h0[2])
+        for i in range(PACK):
+            first_pass(1, 1, banks, i)
+        prepare_w1(1, 2, ("vector", "scalar"))
+        pick_x(0, 3, h0[3])
+        h1 = []
+        for i in range(PACK):
+            first_pass(1, 2, banks, i)
+            h1.append(make_h(1, banks, i))
+        prepare_z(0)
+
+        foam_q = {}
+
+        def prepare_foam(b):
+            grouped = []
+            for half in range(2):
+                g = new_grouped()
+                src = foam_raw[b][:, :, half * HALF : (half + 1) * HALF].rearrange("p j (c e) -> p c j e", e=4)
+                nc.scalar.copy(out=g[:].rearrange("p (c e j) -> p c j e", e=4, j=PACK), in_=src)
+                grouped.append(g)
+            for half in range(2):
+                foam_q[b, half] = quantise(grouped[half], "foam_%d%d" % (b, half))
+
+        pick_x(1, 0, h1[0])
+        prepare_foam(0)
+        pick_x(1, 1, h1[1])
+        pick_x(1, 2, h1[2])
+        prepare_foam(1)
+        pick_x(1, 3, h1[3])
+
+        def second_product(nb, mc, acc, quantised, moving, first):
+            cols = slice((mc % 2) * P, (mc % 2 + 1) * P)
+            for b in range(BLOCKS):
+                codes, scales = quantised[b, mc // 2]
+                nc.tensor.matmul_mx(
+                    out=acc[:],
+                    lhsT=codes[:, cols].bitcast(FP8X4),
+                    lhsT_scale=scales[:, cols],
+                    rhs=moving(b, nb),
+                    rhs_scale=w_planes[first:P, b, nb * BLOCK : (nb + 1) * BLOCK],
+                    start=(b == 0),
+                    stop=(b == BLOCKS - 1),
+                )
+
+        def wf_moving(b, nb):
+            return wf_sb[:, b, nb * BLOCK : (nb + 1) * BLOCK].bitcast(FP8X4)
+
+        def w4_moving(b, nb):
+            return w4_sb[:, b, 2 * nb * BLOCK : 2 * (nb + 1) * BLOCK].bitcast(FP4X4)
+
+        def dealt(acc):
+            return acc[:].rearrange("q (p i) -> q i p", i=PACK)
+
+        def damping(nb, first_bank):
+            tiles = []
+            for pair in range(2):
+                new = []
+                for mc in (2 * pair, 2 * pair + 1):
+                    acc = bank(first_bank + mc)
+                    second_product(nb, mc, acc, foam_q, wf_moving, 4)
+                    d = keep.tile([P, PACK, P], F32, name="damp%d%d" % (nb, mc))
+                    nc.scalar.activation(d[:], dealt(acc), ACT.Abs)
+                    new.append(d)
+                for d in new:
+                    nc.scalar.activation(d[:], d[:], ACT.Abs_reciprocal_sqrt, bias=one[:])
+                for d in new:
+                    nc.scalar.activation(d[:], d[:], ACT.Square)
+                tiles.extend(new)
+            return tiles
+
+        def damp_comfort(nb, damp):
+            for mc in range(4):
+                acc = bank(4 + mc)
+                second_product(nb, mc, acc, z_q, w4_moving, 0)
+                nc.vector.tensor_tensor(damp[mc][:], dealt(acc), damp[mc][:], ALU.mult)
+
+        def make_y(nb, i, damped):
+            acc = bank(i)
+            for mc in range(4):
+                nc.tensor.transpose(acc[:, mc * P : (mc + 1) * P], damped[mc][:, i, :], ident[:])
+            y = ring.tile([P, M], F32, name="y", bufs=3)
+            nc.vector.scalar_tensor_tensor(
+                y[:], x[nb][:, i, :], rho_sb[:, nb, i : i + 1], acc[:], ALU.mult, ALU.add
+            )
+            return y
+
+        out_rows = out.rearrange("(b p i) t -> b i p t", b=BLOCKS, i=PACK)
+
+        def file_y(nb, i, y):
+            nc.vector.tensor_tensor(pages[i][:].indirect(offs3_sb[:]), y[:], wgo_sb[:], ALU.mult)
+            nc.sync.dma_start(out=out_rows[nb, i], in_=pages[i][:])
+
+        damp0 = damping(0, 0)
+        prepare_z(1)
+        damp_comfort(0, damp0)
+        damp1 = damping(1, 4)
+        y = {}
+        y[0] = make_y(0, 0, damp0)
+        for t in range(8):
+            if t == 2:
+                damp_comfort(1, damp1)
+            if t + 1 < 8:
+                nb, i = divmod(t + 1, PACK)
+                y[t + 1] = make_y(nb, i, (damp0, damp1)[nb])
+            nb, i = divmod(t, PACK)
+            file_y(nb, i, y[t])

@@ -60,24 +60,29 @@ def tile_list_mattress_comfort_filing_kernel(
         b1_sb = load_vector(b1, "b1_sb")
         base_sb = load_vector(base, "base_sb")
         rho_sb = load_vector(rho, "rho_sb")
-        for first, scales in ((4, wf_scales), (0, w4_scales)):
+
+        def load_planes(first, scales):
             for q in range(4):
-                nc.gpsimd.dma_start(
+                nc.sync.dma_start(
                     out=w_planes[32 * q + first : 32 * q + first + 4, :, :].bitcast(I32),
                     in_=scales[:, 4 * q : 4 * q + 4, :].bitcast(I32).rearrange("a r n -> r a n"),
                 )
+
         make_identity(nc, ident[:])
 
-        def load_rows(rows):
-            raw = ring.tile([P, PACK, BLOCK], F32, name="raw", bufs=5)
+        def slot(shape, dtype, name):
+            return ring.tile(shape, dtype, name=name, bufs=1, align_bytes=64)
+
+        def load_rows(rows, name):
+            raw = slot([P, PACK, BLOCK], F32, name)
             nc.sync.dma_start(out=raw[:], in_=rows.rearrange("(p j) c -> p j c", j=PACK))
             return raw
 
         def load_w1(b, a):
-            return load_rows(w1[a * BLOCK : (a + 1) * BLOCK, b * BLOCK : (b + 1) * BLOCK])
+            return load_rows(w1[a * BLOCK : (a + 1) * BLOCK, b * BLOCK : (b + 1) * BLOCK], "raw%d%d" % (b, a))
 
         def load_table(a):
-            words = keep.tile([P, T], I32, name="tab%d" % a, align_bytes=64)
+            words = slot([P, T], I32, "big%d" % a)
             nc.sync.dma_start(out=words[:], in_=tab_words[a].rearrange("p t i -> p (t i)").bitcast(I32))
             return words
 
@@ -93,15 +98,22 @@ def tile_list_mattress_comfort_filing_kernel(
         w1_raw[0, 0] = load_w1(0, 0)
         w1_raw[0, 1] = load_w1(0, 1)
         table[1] = load_table(1)
+        table[2] = load_table(2)
+        w1_raw[0, 2] = load_w1(0, 2)
         nc.sync.dma_start(offs2_sb[:], offs2)
         wgt_sb = keep.tile([P, M], F32, name="wgt_sb")
         nc.sync.dma_start(out=wgt_sb[:], in_=wgt)
-        table[2] = load_table(2)
-        w1_raw[0, 2] = load_w1(0, 2)
         for a in range(PASSES):
             w1_raw[1, a] = load_w1(1, a)
+        load_planes(4, wf_scales)
+        w4_sb = keep.tile([P, BLOCKS, 2 * H], U8, name="w4_sb", align_bytes=64)
+        nc.sync.dma_start(out=w4_sb[:].bitcast(I32), in_=w4_words.rearrange("a p c -> p a c").bitcast(I32))
+        load_planes(0, w4_scales)
+        wgo_sb = keep.tile([P, M], F32, name="wgo_sb")
+        nc.sync.dma_start(out=wgo_sb[:], in_=wgo)
+        nc.sync.dma_start(offs3_sb[:], offs3)
 
-        pages = [keep.tile([P, T2], F32, name="page%d" % i) for i in range(PACK)]
+        pages = [keep.tile([P, T2], F32, name="page%d" % i) for i in range(BLOCKS * PACK)]
         for page in pages:
             nc.vector.memset(page[:], 0.0)
 
@@ -111,27 +123,33 @@ def tile_list_mattress_comfort_filing_kernel(
             else:
                 nc.scalar.copy(out=dst, in_=src)
 
-        def quantise(grouped, name):
-            codes = keep.tile([P, HALF], U32, name=name + "_codes", align_bytes=64)
-            scales = keep.tile([P, HALF], U8, name=name + "_scales", align_bytes=64)
-            nc.vector.quantize_mx(out=codes[:].bitcast(FP8X4), scales=scales[:], in_=grouped[:])
+        def quantise(grouped):
+            codes = ring.tile([P, HALF], U32, name="codes", bufs=12, align_bytes=64)
+            scales = ring.tile([P, HALF], U8, name="scales", bufs=12, align_bytes=64)
+            nc.vector.quantize_mx(out=codes[:].bitcast(FP8X4), scales=scales[:], in_=grouped)
             return codes, scales
 
         def new_grouped():
-            return ring.tile([P, HALF * PACK], BF16, name="grouped", bufs=4, align_bytes=64)
+            return ring.tile([P, HALF * PACK], BF16, name="grouped", bufs=3, align_bytes=64)[:]
 
-        def round_w1(b, a, u, engine):
-            grouped = new_grouped()
+        def round_w1(b, a, u, engine, grouped):
             src = w1_raw[b, a][:].rearrange("p j (m i) -> p m j i", i=PACK)[:, :, :, 2 * u : 2 * u + 2]
-            copy_on(engine, grouped[:].rearrange("p (i m j) -> p m j i", i=2, j=PACK), src)
-            return grouped
+            copy_on(engine, grouped.rearrange("p (i m j) -> p m j i", i=2, j=PACK), src)
 
         w1_q = {}
 
-        def prepare_w1(b, a, engines):
-            grouped = [round_w1(b, a, u, engines[u]) for u in range(2)]
-            for u in range(2):
-                w1_q[b, a, u] = quantise(grouped[u], "w1_%d%d%d" % (b, a, u))
+        def prepare_w1(b, units, engine, grouped):
+            for (a, u), g in zip(units, grouped):
+                round_w1(b, a, u, engine, g)
+            for (a, u), g in zip(units, grouped):
+                w1_q[b, a, u] = quantise(g)
+
+        def pair_in(name):
+            pair = slot([P, 2, HALF * PACK], BF16, name)
+            return [pair[:, 0, :], pair[:, 1, :]]
+
+        def single_in(name):
+            return slot([P, HALF * PACK], BF16, name)[:]
 
         picked = {}
 
@@ -156,105 +174,98 @@ def tile_list_mattress_comfort_filing_kernel(
                     stop=(a == PASSES - 1),
                 )
 
-        x = [keep.tile([P, PACK, M], F32, name="x%d" % b) for b in range(BLOCKS)]
+        x = {}
 
-        def make_h(b, banks, i):
-            h = ring.tile([P, S], F32, name="h", bufs=4)
+        def make_h(b, banks, i, name):
+            h = slot([P, S], F32, name)
+            bias = b1_sb[:, b, i : i + 1]
             for half in range(2):
-                nc.scalar.activation(
-                    h[:, half * BANK : (half + 1) * BANK], banks[2 * i + half][:], ACT.Identity,
-                    bias=b1_sb[:, b, i : i + 1],
-                )
+                dst = h[:, half * BANK : (half + 1) * BANK]
+                if (b, i, half) == (0, 0, 1):
+                    nc.vector.tensor_scalar(dst, banks[2 * i + half][:], bias, None, ALU.add)
+                else:
+                    nc.scalar.activation(dst, banks[2 * i + half][:], ACT.Identity, bias=bias)
             return h
 
-        def pick_x(b, i, h):
-            nc.vector.tensor_tensor(x[b][:, i, :], h[:].indirect(offs2_sb[:]), wgt_sb[:], ALU.mult)
+        def pick_x(b, i, h, name=None):
+            x[b, i] = slot([P, M], F32, name or "x%d%d" % (b, i))
+            nc.vector.tensor_tensor(x[b, i][:], h[:].indirect(offs2_sb[:]), wgt_sb[:], ALU.mult)
 
-        def round_z(b, half):
-            grouped = new_grouped()
-            src = x[b][:, :, half * HALF : (half + 1) * HALF].rearrange("p i (c e) -> p c i e", e=4)
-            floor = base_sb[:, b, :].unsqueeze(1).unsqueeze(3).to_broadcast([P, HALF // 4, PACK, 4])
-            nc.vector.tensor_tensor(
-                grouped[:].rearrange("p (c e i) -> p c i e", e=4, i=PACK), src, floor, ALU.max
+        z_planes = {}
+
+        def floor_x(b, i):
+            nc.vector.tensor_scalar(
+                z_planes[b][:, i, :], x[b, i][:], base_sb[:, b, i : i + 1], None, ALU.max
             )
+
+        def interleave(engine, planes, half, grouped):
+            src = planes[:, :, half * HALF : (half + 1) * HALF].rearrange("p j (c e) -> p c j e", e=4)
+            copy_on(engine, grouped.rearrange("p (c e j) -> p c j e", e=4, j=PACK), src)
             return grouped
-
-        z_q = {}
-
-        def prepare_z(b):
-            grouped = [round_z(b, half) for half in range(2)]
-            for half in range(2):
-                z_q[b, half] = quantise(grouped[half], "z_%d%d" % (b, half))
 
         pick_words(0)
         nc.vector.tensor_copy(out=picked_planes[:], in_=tab_planes[:].indirect(offs_sb[:]))
-        prepare_w1(0, 0, ("scalar", "scalar"))
+        prepare_w1(0, [(0, 0), (0, 1)], "scalar", [new_grouped(), new_grouped()])
         banks = [bank(k) for k in range(8)]
         for i in range(PACK):
             first_pass(0, 0, banks, i)
-        prepare_w1(0, 1, ("scalar", "scalar"))
+        prepare_w1(0, [(1, 0), (1, 1)], "scalar", [new_grouped(), new_grouped()])
         pick_words(1)
         for i in range(PACK):
             first_pass(0, 1, banks, i)
         pick_words(2)
-        prepare_w1(0, 2, ("vector", "scalar"))
+        foam_raw = [load_rows(foam[b * BLOCK : (b + 1) * BLOCK, :], "big%d" % b) for b in range(BLOCKS)]
+
+        grouped = [single_in("big2"), new_grouped()]
+        round_w1(0, 2, 0, "vector", grouped[0])
+        round_w1(0, 2, 1, "scalar", grouped[1])
+        for u in range(2):
+            w1_q[0, 2, u] = quantise(grouped[u])
         h0 = []
         for i in range(PACK):
             first_pass(0, 2, banks, i)
-            h0.append(make_h(0, banks, i))
-
-        foam_raw = [load_rows(foam[b * BLOCK : (b + 1) * BLOCK, :]) for b in range(BLOCKS)]
-        wf_sb = keep.tile([P, BLOCKS, H], I32, name="wf_sb", align_bytes=64)
-        nc.sync.dma_start(out=wf_sb[:], in_=wf_words.rearrange("a p c i -> p a (c i)").bitcast(I32))
-        w4_sb = keep.tile([P, BLOCKS, 2 * H], U8, name="w4_sb", align_bytes=64)
-        nc.sync.dma_start(out=w4_sb[:].bitcast(I32), in_=w4_words.rearrange("a p c -> p a c").bitcast(I32))
-        nc.sync.dma_start(offs3_sb[:], offs3)
-        wgo_sb = keep.tile([P, M], F32, name="wgo_sb")
-        nc.sync.dma_start(out=wgo_sb[:], in_=wgo)
+            h0.append(make_h(0, banks, i, "h%d" % i))
 
         banks = [bank(k) for k in range(8)]
-        prepare_w1(1, 0, ("vector", "vector"))
-        pick_x(0, 0, h0[0])
-        pick_x(0, 1, h0[1])
+        prepare_w1(1, [(0, 0), (0, 1)], "vector", pair_in("big2"))
         for i in range(PACK):
+            pick_x(0, i, h0[i])
             first_pass(1, 0, banks, i)
-        prepare_w1(1, 1, ("scalar", "scalar"))
-        pick_x(0, 2, h0[2])
-        for i in range(PACK):
-            first_pass(1, 1, banks, i)
-        prepare_w1(1, 2, ("vector", "scalar"))
-        pick_x(0, 3, h0[3])
+        prepare_w1(1, [(1, 0), (2, 0)], "scalar", pair_in("big2"))
+        wf_sb = slot([P, BLOCKS, H], I32, "big2")
+        nc.sync.dma_start(out=wf_sb[:], in_=wf_words.rearrange("a p c i -> p a (c i)").bitcast(I32))
+        prepare_w1(1, [(1, 1), (2, 1)], "scalar", [single_in("h0"), single_in("h1")])
         h1 = []
         for i in range(PACK):
+            first_pass(1, 1, banks, i)
             first_pass(1, 2, banks, i)
-            h1.append(make_h(1, banks, i))
-        prepare_z(0)
+            h1.append(make_h(1, banks, i, ("raw00", "raw01", "h2", "h3")[i]))
+        z_planes[0] = slot([P, PACK, M], BF16, "h1")
+        z_planes[1] = slot([P, PACK, M], BF16, "h0")
+        for i in range(PACK):
+            floor_x(0, i)
 
         foam_q = {}
+        z_q = {}
 
-        def prepare_foam(b):
-            grouped = []
-            for half in range(2):
-                g = new_grouped()
-                src = foam_raw[b][:, :, half * HALF : (half + 1) * HALF].rearrange("p j (c e) -> p c j e", e=4)
-                nc.scalar.copy(out=g[:].rearrange("p (c e j) -> p c j e", e=4, j=PACK), in_=src)
-                grouped.append(g)
-            for half in range(2):
-                foam_q[b, half] = quantise(grouped[half], "foam_%d%d" % (b, half))
-
-        pick_x(1, 0, h1[0])
-        prepare_foam(0)
-        pick_x(1, 1, h1[1])
-        pick_x(1, 2, h1[2])
-        prepare_foam(1)
-        pick_x(1, 3, h1[3])
-
-        def second_product(nb, mc, acc, quantised, moving, first):
-            cols = slice((mc % 2) * P, (mc % 2 + 1) * P)
+        def prepare_foam(half, grouped):
             for b in range(BLOCKS):
-                codes, scales = quantised[b, mc // 2]
+                interleave("scalar", foam_raw[b], half, grouped[b])
+            for b in range(BLOCKS):
+                foam_q[b, half] = quantise(grouped[b])
+
+        def wf_moving(b, nb):
+            return wf_sb[:, b, nb * BLOCK : (nb + 1) * BLOCK].bitcast(FP8X4)
+
+        def w4_moving(b, nb):
+            return w4_sb[:, b, 2 * nb * BLOCK : 2 * (nb + 1) * BLOCK].bitcast(FP4X4)
+
+        def second_pass(nb, half, b, accs, quantised, moving, first):
+            codes, scales = quantised[b, half]
+            for c in range(2):
+                cols = slice(c * P, (c + 1) * P)
                 nc.tensor.matmul_mx(
-                    out=acc[:],
+                    out=accs[c][:],
                     lhsT=codes[:, cols].bitcast(FP8X4),
                     lhsT_scale=scales[:, cols],
                     rhs=moving(b, nb),
@@ -263,65 +274,98 @@ def tile_list_mattress_comfort_filing_kernel(
                     stop=(b == BLOCKS - 1),
                 )
 
-        def wf_moving(b, nb):
-            return wf_sb[:, b, nb * BLOCK : (nb + 1) * BLOCK].bitcast(FP8X4)
-
-        def w4_moving(b, nb):
-            return w4_sb[:, b, 2 * nb * BLOCK : 2 * (nb + 1) * BLOCK].bitcast(FP4X4)
-
         def dealt(acc):
             return acc[:].rearrange("q (p i) -> q i p", i=PACK)
 
-        def damping(nb, first_bank):
-            tiles = []
-            for pair in range(2):
-                new = []
-                for mc in (2 * pair, 2 * pair + 1):
-                    acc = bank(first_bank + mc)
-                    second_product(nb, mc, acc, foam_q, wf_moving, 4)
-                    d = keep.tile([P, PACK, P], F32, name="damp%d%d" % (nb, mc))
-                    nc.scalar.activation(d[:], dealt(acc), ACT.Abs)
-                    new.append(d)
-                for d in new:
-                    nc.scalar.activation(d[:], d[:], ACT.Abs_reciprocal_sqrt, bias=one[:])
-                for d in new:
-                    nc.scalar.activation(d[:], d[:], ACT.Square)
-                tiles.extend(new)
-            return tiles
+        phases = [(nb, half) for half in range(2) for nb in range(BLOCKS)]
 
-        def damp_comfort(nb, damp):
-            for mc in range(4):
-                acc = bank(4 + mc)
-                second_product(nb, mc, acc, z_q, w4_moving, 0)
-                nc.vector.tensor_tensor(damp[mc][:], dealt(acc), damp[mc][:], ALU.mult)
+        def damping(ph):
+            nb, half = phases[ph]
+            accs = [bank(c) for c in range(2)]
+            for b in range(BLOCKS):
+                second_pass(nb, half, b, accs, foam_q, wf_moving, 4)
+            damp = [ring.tile([P, PACK, P], F32, name="shared%d%d" % (ph % 2, c), bufs=1) for c in range(2)]
+            for c in range(2):
+                nc.scalar.activation(damp[c][:], dealt(accs[c]), ACT.Abs)
+            for d in damp:
+                nc.scalar.activation(d[:], d[:], ACT.Abs_reciprocal_sqrt, bias=one[:])
+                nc.scalar.activation(d[:], d[:], ACT.Square)
+            return damp
 
-        def make_y(nb, i, damped):
-            acc = bank(i)
-            for mc in range(4):
-                nc.tensor.transpose(acc[:, mc * P : (mc + 1) * P], damped[mc][:, i, :], ident[:])
-            y = ring.tile([P, M], F32, name="y", bufs=3)
+        def comfort_pass(ph, b, accs):
+            nb, half = phases[ph]
+            second_pass(nb, half, b, accs, z_q, w4_moving, 0)
+
+        def damp_comfort(accs, damp):
+            damped = []
+            for c in range(2):
+                t = ring.tile([P, PACK, P], F32, name="damped", bufs=4)
+                nc.vector.tensor_tensor(t[:], dealt(accs[c]), damp[c][:], ALU.mult)
+                damped.append(t)
+            return damped
+
+        def make_y(ph, i, damped):
+            nb, half = phases[ph]
+            acc = bank(4 + i)
+            for c in range(2):
+                nc.tensor.transpose(acc[:, c * P : (c + 1) * P], damped[c][:, i, :], ident[:])
+            if i >= 2 and ph + 1 < len(phases):
+                y = ring.tile([P, HALF], F32, name="shared%d%d" % ((ph + 1) % 2, i - 2), bufs=1)
+            else:
+                y = ring.tile([P, HALF], F32, name="y", bufs=3)
             nc.vector.scalar_tensor_tensor(
-                y[:], x[nb][:, i, :], rho_sb[:, nb, i : i + 1], acc[:], ALU.mult, ALU.add
+                y[:], x[nb, i][:, half * HALF : (half + 1) * HALF], rho_sb[:, nb, i : i + 1],
+                acc[:, 0:HALF], ALU.mult, ALU.add,
             )
             return y
 
         out_rows = out.rearrange("(b p i) t -> b i p t", b=BLOCKS, i=PACK)
 
-        def file_y(nb, i, y):
-            nc.vector.tensor_tensor(pages[i][:].indirect(offs3_sb[:]), y[:], wgo_sb[:], ALU.mult)
-            nc.sync.dma_start(out=out_rows[nb, i], in_=pages[i][:])
+        def file_y(ph, i, y):
+            nb, half = phases[ph]
+            page = pages[nb * PACK + i]
+            places = offs3_sb[:, half * (HALF // 16) : (half + 1) * (HALF // 16)]
+            nc.vector.tensor_tensor(
+                page[:].indirect(places), y[:], wgo_sb[:, half * HALF : (half + 1) * HALF], ALU.mult
+            )
+            if half == 1:
+                nc.sync.dma_start(out=out_rows[nb, i], in_=page[:])
 
-        damp0 = damping(0, 0)
-        prepare_z(1)
-        damp_comfort(0, damp0)
-        damp1 = damping(1, 4)
-        y = {}
-        y[0] = make_y(0, 0, damp0)
-        for t in range(8):
-            if t == 2:
-                damp_comfort(1, damp1)
-            if t + 1 < 8:
-                nb, i = divmod(t + 1, PACK)
-                y[t + 1] = make_y(nb, i, (damp0, damp1)[nb])
-            nb, i = divmod(t, PACK)
-            file_y(nb, i, y[t])
+        pick_x(1, 0, h1[0])
+        grouped = interleave("vector", z_planes[0], 0, new_grouped())
+        pick_x(1, 1, h1[1])
+        z_q[0, 0] = quantise(grouped)
+        floor_x(1, 0)
+        accs = [bank(2 + c) for c in range(2)]
+        comfort_pass(0, 0, accs)
+        prepare_foam(0, [single_in("raw00"), single_in("raw01")])
+        pick_x(1, 2, h1[2])
+        floor_x(1, 1)
+        floor_x(1, 2)
+        pick_x(1, 3, h1[3], "raw01")
+        damp = damping(0)
+        floor_x(1, 3)
+        z_q[1, 0] = quantise(interleave("vector", z_planes[1], 0, new_grouped()))
+        comfort_pass(0, 1, accs)
+        damped = damp_comfort(accs, damp)
+
+        for ph in range(len(phases)):
+            ys = [make_y(ph, i, damped) for i in range(2)]
+            file_y(ph, 0, ys[0])
+            if ph + 1 < len(phases):
+                damp = damping(ph + 1)
+                if ph == 0:
+                    prepare_foam(1, [single_in("h2"), single_in("h3")])
+                    grouped = [interleave("scalar", z_planes[b], 1, new_grouped()) for b in range(BLOCKS)]
+                    for b in range(BLOCKS):
+                        z_q[b, 1] = quantise(grouped[b])
+                accs = [bank(2 + c) for c in range(2)]
+                for b in range(BLOCKS):
+                    comfort_pass(ph + 1, b, accs)
+            file_y(ph, 1, ys[1])
+            if ph + 1 < len(phases):
+                next_damped = damp_comfort(accs, damp)
+            ys = [make_y(ph, i, damped) for i in range(2, PACK)]
+            file_y(ph, 2, ys[0])
+            file_y(ph, 3, ys[1])
+            damped = next_damped

@@ -39,6 +39,9 @@ def tile_list_mattress_comfort_filing_kernel(
         def bank(k):
             return psum.tile([P, BANK], F32, name="bank%d" % k)
 
+        def slot(shape, dtype, name):
+            return ring.tile(shape, dtype, name=name, bufs=1, align_bytes=64)
+
         offs_sb = keep.tile([P, S // 16], U16, name="offs_sb")
         offs2_sb = keep.tile([P, M // 16], U16, name="offs2_sb")
         offs3_sb = keep.tile([P, M // 16], U16, name="offs3_sb")
@@ -53,7 +56,7 @@ def tile_list_mattress_comfort_filing_kernel(
         nc.scalar.activation(warm[:], one[:], ACT.Abs_reciprocal_sqrt, bias=one[:])
 
         def load_vector(vec, name):
-            sb = keep.tile([P, BLOCKS, PACK], F32, name=name)
+            sb = slot([P, BLOCKS, PACK], F32, name)
             nc.gpsimd.dma_start(out=sb[:], in_=vec.rearrange("(b p i) -> p b i", b=BLOCKS, i=PACK))
             return sb
 
@@ -69,9 +72,6 @@ def tile_list_mattress_comfort_filing_kernel(
                 )
 
         make_identity(nc, ident[:])
-
-        def slot(shape, dtype, name):
-            return ring.tile(shape, dtype, name=name, bufs=1, align_bytes=64)
 
         def load_rows(rows, name):
             raw = slot([P, PACK, BLOCK], F32, name)
@@ -100,10 +100,11 @@ def tile_list_mattress_comfort_filing_kernel(
         table[1] = load_table(1)
         table[2] = load_table(2)
         w1_raw[0, 2] = load_w1(0, 2)
+        w1_raw[1, 0] = load_w1(1, 0)
         nc.sync.dma_start(offs2_sb[:], offs2)
         wgt_sb = keep.tile([P, M], F32, name="wgt_sb")
         nc.sync.dma_start(out=wgt_sb[:], in_=wgt)
-        for a in range(PASSES):
+        for a in range(1, PASSES):
             w1_raw[1, a] = load_w1(1, a)
         load_planes(4, wf_scales)
         w4_sb = keep.tile([P, BLOCKS, 2 * H], U8, name="w4_sb", align_bytes=64)
@@ -124,13 +125,21 @@ def tile_list_mattress_comfort_filing_kernel(
                 nc.scalar.copy(out=dst, in_=src)
 
         def quantise(grouped):
-            codes = ring.tile([P, HALF], U32, name="codes", bufs=12, align_bytes=64)
-            scales = ring.tile([P, HALF], U8, name="scales", bufs=12, align_bytes=64)
+            codes = ring.tile([P, HALF], U32, name="codes", bufs=4, align_bytes=64)
+            scales = ring.tile([P, HALF], U8, name="scales", bufs=4, align_bytes=64)
             nc.vector.quantize_mx(out=codes[:].bitcast(FP8X4), scales=scales[:], in_=grouped)
-            return codes, scales
+            return codes[:], scales[:]
+
+        def quantise_pair(pair):
+            codes = ring.tile([P, 2 * HALF], U32, name="codes2", bufs=6, align_bytes=64)
+            scales = ring.tile([P, 2 * HALF], U8, name="scales2", bufs=6, align_bytes=64)
+            nc.vector.quantize_mx(
+                out=codes[:].bitcast(FP8X4), scales=scales[:], in_=pair[:].rearrange("p e n -> p (e n)")
+            )
+            return [(codes[:, e * HALF : (e + 1) * HALF], scales[:, e * HALF : (e + 1) * HALF]) for e in range(2)]
 
         def new_grouped():
-            return ring.tile([P, HALF * PACK], BF16, name="grouped", bufs=3, align_bytes=64)[:]
+            return ring.tile([P, HALF * PACK], BF16, name="grouped", bufs=2, align_bytes=64)[:]
 
         def round_w1(b, a, u, engine, grouped):
             src = w1_raw[b, a][:].rearrange("p j (m i) -> p m j i", i=PACK)[:, :, :, 2 * u : 2 * u + 2]
@@ -138,18 +147,18 @@ def tile_list_mattress_comfort_filing_kernel(
 
         w1_q = {}
 
-        def prepare_w1(b, units, engine, grouped):
-            for (a, u), g in zip(units, grouped):
-                round_w1(b, a, u, engine, g)
-            for (a, u), g in zip(units, grouped):
-                w1_q[b, a, u] = quantise(g)
-
         def pair_in(name):
-            pair = slot([P, 2, HALF * PACK], BF16, name)
-            return [pair[:, 0, :], pair[:, 1, :]]
+            return slot([P, 2, HALF * PACK], BF16, name)
 
         def single_in(name):
             return slot([P, HALF * PACK], BF16, name)[:]
+
+        def prepare_w1(b, units, engine, name):
+            pair = pair_in(name)
+            for e, (a, u) in enumerate(units):
+                round_w1(b, a, u, engine, pair[:, e, :])
+            for (a, u), q in zip(units, quantise_pair(pair)):
+                w1_q[b, a, u] = q
 
         picked = {}
 
@@ -187,15 +196,30 @@ def tile_list_mattress_comfort_filing_kernel(
                     nc.scalar.activation(dst, banks[2 * i + half][:], ACT.Identity, bias=bias)
             return h
 
-        def pick_x(b, i, h, name=None):
-            x[b, i] = slot([P, M], F32, name or "x%d%d" % (b, i))
-            nc.vector.tensor_tensor(x[b, i][:], h[:].indirect(offs2_sb[:]), wgt_sb[:], ALU.mult)
+        def pick_x(b, i, h):
+            whole = slot([P, M], F32, "x%d%d" % (b, i))
+            nc.vector.tensor_tensor(whole[:], h[:].indirect(offs2_sb[:]), wgt_sb[:], ALU.mult)
+            x[b, i] = whole[:]
+            for half in range(2):
+                x[b, i, half] = whole[:, half * HALF : (half + 1) * HALF]
+
+        def pick_x_half(b, i, half, h, name):
+            part = slot([P, HALF], F32, name)
+            entries = offs2_sb[:, half * (HALF // 16) : (half + 1) * (HALF // 16)]
+            nc.vector.tensor_tensor(
+                part[:], h[:].indirect(entries), wgt_sb[:, half * HALF : (half + 1) * HALF], ALU.mult
+            )
+            x[b, i, half] = part[:]
 
         z_planes = {}
 
         def floor_x(b, i):
+            nc.vector.tensor_scalar(z_planes[b][:, i, :], x[b, i], base_sb[:, b, i : i + 1], None, ALU.max)
+
+        def floor_x_half(b, i, half):
             nc.vector.tensor_scalar(
-                z_planes[b][:, i, :], x[b, i][:], base_sb[:, b, i : i + 1], None, ALU.max
+                z_planes[b][:, i, half * HALF : (half + 1) * HALF], x[b, i, half],
+                base_sb[:, b, i : i + 1], None, ALU.max,
             )
 
         def interleave(engine, planes, half, grouped):
@@ -205,11 +229,11 @@ def tile_list_mattress_comfort_filing_kernel(
 
         pick_words(0)
         nc.vector.tensor_copy(out=picked_planes[:], in_=tab_planes[:].indirect(offs_sb[:]))
-        prepare_w1(0, [(0, 0), (0, 1)], "scalar", [new_grouped(), new_grouped()])
+        prepare_w1(0, [(0, 0), (0, 1)], "scalar", "h2")
         banks = [bank(k) for k in range(8)]
         for i in range(PACK):
             first_pass(0, 0, banks, i)
-        prepare_w1(0, [(1, 0), (1, 1)], "scalar", [new_grouped(), new_grouped()])
+        prepare_w1(0, [(1, 0), (1, 1)], "scalar", "h3")
         pick_words(1)
         for i in range(PACK):
             first_pass(0, 1, banks, i)
@@ -227,32 +251,32 @@ def tile_list_mattress_comfort_filing_kernel(
             h0.append(make_h(0, banks, i, "h%d" % i))
 
         banks = [bank(k) for k in range(8)]
-        prepare_w1(1, [(0, 0), (0, 1)], "vector", pair_in("big2"))
+        prepare_w1(1, [(0, 0), (0, 1)], "vector", "big2")
         for i in range(PACK):
             pick_x(0, i, h0[i])
             first_pass(1, 0, banks, i)
-        prepare_w1(1, [(1, 0), (2, 0)], "scalar", pair_in("big2"))
+        prepare_w1(1, [(1, 0), (2, 0)], "scalar", "big2")
         wf_sb = slot([P, BLOCKS, H], I32, "big2")
         nc.sync.dma_start(out=wf_sb[:], in_=wf_words.rearrange("a p c i -> p a (c i)").bitcast(I32))
-        prepare_w1(1, [(1, 1), (2, 1)], "scalar", [single_in("h0"), single_in("h1")])
+        prepare_w1(1, [(1, 1), (2, 1)], "scalar", "h1")
         h1 = []
         for i in range(PACK):
             first_pass(1, 1, banks, i)
             first_pass(1, 2, banks, i)
             h1.append(make_h(1, banks, i, ("raw00", "raw01", "h2", "h3")[i]))
         z_planes[0] = slot([P, PACK, M], BF16, "h1")
-        z_planes[1] = slot([P, PACK, M], BF16, "h0")
         for i in range(PACK):
             floor_x(0, i)
 
         foam_q = {}
         z_q = {}
 
-        def prepare_foam(half, grouped):
+        def prepare_half(planes, half, name, quantised):
+            pair = pair_in(name)
             for b in range(BLOCKS):
-                interleave("scalar", foam_raw[b], half, grouped[b])
-            for b in range(BLOCKS):
-                foam_q[b, half] = quantise(grouped[b])
+                interleave("scalar", planes[b], half, pair[:, b, :])
+            for b, q in enumerate(quantise_pair(pair)):
+                quantised[b, half] = q
 
         def wf_moving(b, nb):
             return wf_sb[:, b, nb * BLOCK : (nb + 1) * BLOCK].bitcast(FP8X4)
@@ -260,19 +284,18 @@ def tile_list_mattress_comfort_filing_kernel(
         def w4_moving(b, nb):
             return w4_sb[:, b, 2 * nb * BLOCK : 2 * (nb + 1) * BLOCK].bitcast(FP4X4)
 
-        def second_pass(nb, half, b, accs, quantised, moving, first):
+        def second_pass(nb, half, b, c, acc, quantised, moving, first):
             codes, scales = quantised[b, half]
-            for c in range(2):
-                cols = slice(c * P, (c + 1) * P)
-                nc.tensor.matmul_mx(
-                    out=accs[c][:],
-                    lhsT=codes[:, cols].bitcast(FP8X4),
-                    lhsT_scale=scales[:, cols],
-                    rhs=moving(b, nb),
-                    rhs_scale=w_planes[first:P, b, nb * BLOCK : (nb + 1) * BLOCK],
-                    start=(b == 0),
-                    stop=(b == BLOCKS - 1),
-                )
+            cols = slice(c * P, (c + 1) * P)
+            nc.tensor.matmul_mx(
+                out=acc[:],
+                lhsT=codes[:, cols].bitcast(FP8X4),
+                lhsT_scale=scales[:, cols],
+                rhs=moving(b, nb),
+                rhs_scale=w_planes[first:P, b, nb * BLOCK : (nb + 1) * BLOCK],
+                start=(b == 0),
+                stop=(b == BLOCKS - 1),
+            )
 
         def dealt(acc):
             return acc[:].rearrange("q (p i) -> q i p", i=PACK)
@@ -282,41 +305,73 @@ def tile_list_mattress_comfort_filing_kernel(
         def damping(ph):
             nb, half = phases[ph]
             accs = [bank(c) for c in range(2)]
-            for b in range(BLOCKS):
-                second_pass(nb, half, b, accs, foam_q, wf_moving, 4)
-            damp = [ring.tile([P, PACK, P], F32, name="shared%d%d" % (ph % 2, c), bufs=1) for c in range(2)]
+            for c in range(2):
+                for b in range(BLOCKS):
+                    second_pass(nb, half, b, c, accs[c], foam_q, wf_moving, 4)
+            damp = [ring.tile([P, PACK, P], F32, name="damp", bufs=4) for c in range(2)]
             for c in range(2):
                 nc.scalar.activation(damp[c][:], dealt(accs[c]), ACT.Abs)
-            for d in damp:
-                nc.scalar.activation(d[:], d[:], ACT.Abs_reciprocal_sqrt, bias=one[:])
-                nc.scalar.activation(d[:], d[:], ACT.Square)
+            for c in range(2):
+                root = slot([P, PACK, P], F32, "first_root" if (ph, c) == (0, 0) else "root%d" % c)
+                nc.scalar.activation(root[:], damp[c][:], ACT.Abs_reciprocal_sqrt, bias=one[:])
+                nc.scalar.activation(damp[c][:], root[:], ACT.Square)
             return damp
 
         def comfort_pass(ph, b, accs):
             nb, half = phases[ph]
-            second_pass(nb, half, b, accs, z_q, w4_moving, 0)
-
-        def damp_comfort(accs, damp):
-            damped = []
             for c in range(2):
-                t = ring.tile([P, PACK, P], F32, name="damped", bufs=4)
-                nc.vector.tensor_tensor(t[:], dealt(accs[c]), damp[c][:], ALU.mult)
-                damped.append(t)
-            return damped
+                second_pass(nb, half, b, c, accs[c], z_q, w4_moving, 0)
 
-        def make_y(ph, i, damped):
+        def damp_comfort(acc, damp):
+            nc.vector.tensor_tensor(damp[:], dealt(acc), damp[:], ALU.mult)
+
+        def x_half(ph, i):
             nb, half = phases[ph]
-            acc = bank(4 + i)
+            return x[nb, i, half]
+
+        def turn_residual(ph):
+            nb = phases[ph][0]
+            accs = [bank(6 + c) for c in range(2)]
+            for i in range(PACK):
+                scaled = ring.tile([P, HALF], F32, name="scaled", bufs=4)
+                nc.scalar.activation(scaled[:], x_half(ph, i), ACT.Copy, scale=rho_sb[:, nb, i : i + 1])
+                for c in range(2):
+                    nc.tensor.transpose(accs[c][:, i * P : (i + 1) * P], scaled[:, c * P : (c + 1) * P], ident[:])
+            return accs
+
+        def fetch_residual(ph, accs):
+            turned = []
             for c in range(2):
-                nc.tensor.transpose(acc[:, c * P : (c + 1) * P], damped[c][:, i, :], ident[:])
-            if i >= 2 and ph + 1 < len(phases):
-                y = ring.tile([P, HALF], F32, name="shared%d%d" % ((ph + 1) % 2, i - 2), bufs=1)
+                t = slot([P, PACK, P], F32, ("raw02", "raw10", "raw11", "raw12")[2 * (ph % 2) + c])
+                nc.scalar.copy(out=t[:].rearrange("q i p -> q (i p)"), in_=accs[c][:])
+                turned.append(t)
+            return turned
+
+        def make_y(ph, pair, damped, turned):
+            nb = phases[ph][0]
+            acc = bank(4 + pair)
+            if pair == 1 and ph + 1 < len(phases):
+                y = slot([P, 2, HALF], F32, "root1")
             else:
-                y = ring.tile([P, HALF], F32, name="y", bufs=3)
-            nc.vector.scalar_tensor_tensor(
-                y[:], x[nb, i][:, half * HALF : (half + 1) * HALF], rho_sb[:, nb, i : i + 1],
-                acc[:, 0:HALF], ALU.mult, ALU.add,
-            )
+                y = ring.tile([P, 2, HALF], F32, name="y", bufs=2)
+            for e in range(2):
+                i = 2 * pair + e
+                for c in range(2):
+                    dst = acc[:, e * HALF + c * P : e * HALF + (c + 1) * P]
+                    if turned is None:
+                        nc.tensor.transpose(dst, damped[c][:, i, :], ident[:])
+                    else:
+                        nc.tensor.matmul(dst, damped[c][:, i, :], ident[:], start=True, stop=False, is_transpose=True)
+                        nc.tensor.matmul(dst, turned[c][:, i, :], ident[:], start=False, stop=True, is_transpose=True)
+            if turned is None:
+                for e in range(2):
+                    i = 2 * pair + e
+                    nc.vector.scalar_tensor_tensor(
+                        y[:, e, :], x_half(ph, i), rho_sb[:, nb, i : i + 1],
+                        acc[:, e * HALF : (e + 1) * HALF], ALU.mult, ALU.add,
+                    )
+            else:
+                nc.scalar.copy(out=y[:].rearrange("p e m -> p (e m)"), in_=acc[:])
             return y
 
         out_rows = out.rearrange("(b p i) t -> b i p t", b=BLOCKS, i=PACK)
@@ -326,7 +381,7 @@ def tile_list_mattress_comfort_filing_kernel(
             page = pages[nb * PACK + i]
             places = offs3_sb[:, half * (HALF // 16) : (half + 1) * (HALF // 16)]
             nc.vector.tensor_tensor(
-                page[:].indirect(places), y[:], wgo_sb[:, half * HALF : (half + 1) * HALF], ALU.mult
+                page[:].indirect(places), y, wgo_sb[:, half * HALF : (half + 1) * HALF], ALU.mult
             )
             if half == 1:
                 nc.sync.dma_start(out=out_rows[nb, i], in_=page[:])
@@ -335,37 +390,48 @@ def tile_list_mattress_comfort_filing_kernel(
         grouped = interleave("vector", z_planes[0], 0, new_grouped())
         pick_x(1, 1, h1[1])
         z_q[0, 0] = quantise(grouped)
-        floor_x(1, 0)
         accs = [bank(2 + c) for c in range(2)]
         comfort_pass(0, 0, accs)
-        prepare_foam(0, [single_in("raw00"), single_in("raw01")])
-        pick_x(1, 2, h1[2])
+        prepare_half(foam_raw, 0, "b1_sb", foam_q)
+        z_planes[1] = slot([P, PACK, M], BF16, "h0")
+        floor_x(1, 0)
         floor_x(1, 1)
-        floor_x(1, 2)
-        pick_x(1, 3, h1[3], "raw01")
+        pick_x_half(1, 2, 0, h1[2], "b1_sb")
+        pick_x_half(1, 3, 0, h1[3], "x130")
         damp = damping(0)
-        floor_x(1, 3)
-        z_q[1, 0] = quantise(interleave("vector", z_planes[1], 0, new_grouped()))
+        floor_x_half(1, 2, 0)
+        floor_x_half(1, 3, 0)
+        z_q[1, 0] = quantise(interleave("vector", z_planes[1], 0, single_in("raw00")))
         comfort_pass(0, 1, accs)
-        damped = damp_comfort(accs, damp)
+        pick_x_half(1, 2, 1, h1[2], "raw00")
+        damp_comfort(accs[0], damp[0])
+        pick_x_half(1, 3, 1, h1[3], "first_root")
+        damp_comfort(accs[1], damp[1])
+        floor_x_half(1, 2, 1)
+        floor_x_half(1, 3, 1)
 
-        for ph in range(len(phases)):
-            ys = [make_y(ph, i, damped) for i in range(2)]
-            file_y(ph, 0, ys[0])
-            if ph + 1 < len(phases):
-                damp = damping(ph + 1)
-                if ph == 0:
-                    prepare_foam(1, [single_in("h2"), single_in("h3")])
-                    grouped = [interleave("scalar", z_planes[b], 1, new_grouped()) for b in range(BLOCKS)]
-                    for b in range(BLOCKS):
-                        z_q[b, 1] = quantise(grouped[b])
-                accs = [bank(2 + c) for c in range(2)]
-                for b in range(BLOCKS):
-                    comfort_pass(ph + 1, b, accs)
-            file_y(ph, 1, ys[1])
-            if ph + 1 < len(phases):
-                next_damped = damp_comfort(accs, damp)
-            ys = [make_y(ph, i, damped) for i in range(2, PACK)]
-            file_y(ph, 2, ys[0])
-            file_y(ph, 3, ys[1])
-            damped = next_damped
+        turned = None
+        y = make_y(0, 0, damp, turned)
+        for ph in range(len(phases) - 1):
+            file_y(ph, 0, y[:, 0, :])
+            residual = turn_residual(ph + 1)
+            next_damp = damping(ph + 1)
+            accs = [bank(2 + c) for c in range(2)]
+            for b in range(BLOCKS):
+                comfort_pass(ph + 1, b, accs)
+            file_y(ph, 1, y[:, 1, :])
+            for c in range(2):
+                damp_comfort(accs[c], next_damp[c])
+            y = make_y(ph, 1, damp, turned)
+            turned = fetch_residual(ph + 1, residual)
+            file_y(ph, 2, y[:, 0, :])
+            file_y(ph, 3, y[:, 1, :])
+            if ph == 0:
+                prepare_half(foam_raw, 1, "raw01", foam_q)
+                prepare_half(z_planes, 1, "h3", z_q)
+            damp = next_damp
+            y = make_y(ph + 1, 0, damp, turned)
+        last = len(phases) - 1
+        y_rest = make_y(last, 1, damp, turned)
+        for i in range(PACK):
+            file_y(last, i, (y, y_rest)[i // 2][:, i % 2, :])

from contextlib import ExitStack

import concourse.mybir as mybir
from concourse.masks import make_identity

T, S, M, T2, K, H = 4096, 1024, 512, 1024, 1536, 1024
FLOPS = 2 * (K * H * S + 2 * H * H * M)

F32 = mybir.dt.float32
BF16 = mybir.dt.bfloat16
I32 = mybir.dt.int32
U32 = mybir.dt.uint32
U16 = mybir.dt.uint16
U8 = mybir.dt.uint8
FP8X4 = mybir.dt.float8_e4m3fn_x4
FP4X4 = mybir.dt.float4_e2m1fn_x4
ALU = mybir.AluOpType
ACT = mybir.ActivationFunctionType

P = 128
PACK = 4
BLOCK = P * PACK
PASSES = K // BLOCK
BLOCKS = H // BLOCK
BANK = 512
HALF = 256


def tile_list_mattress_comfort_filing_kernel(
    tc, tab_words, tab_scales, offs, w1, b1, offs2, wgt, base, w4_words, w4_scales,
    foam, wf_words, wf_scales, rho, offs3, wgo, out,
):
    nc = tc.nc
    with ExitStack() as ctx:
        keep = ctx.enter_context(tc.tile_pool(name="keep", bufs=1))
        ring = ctx.enter_context(tc.tile_pool(name="ring", bufs=1))
        psum = ctx.enter_context(tc.psum_pool(name="psum", bufs=1))

        def bank(k):
            return psum.tile([P, BANK], F32, name="bank%d" % k)

        def slot(shape, dtype, name):
            return ring.tile(shape, dtype, name=name, bufs=1, align_bytes=64)

        offs_sb = keep.tile([P, S // 16], U16, name="offs_sb")
        offs2_sb = keep.tile([P, M // 16], U16, name="offs2_sb")
        offs3_sb = keep.tile([P, M // 16], U16, name="offs3_sb")
        tab_planes = keep.tile([P, T], U8, name="tab_planes", align_bytes=64)
        w_planes = keep.tile([P, BLOCKS, H], U8, name="w_planes", align_bytes=64)
        one = keep.tile([P, 1], F32, name="one")
        warm = keep.tile([P, 1], F32, name="warm")
        ident = keep.tile([P, P], F32, name="ident")
        nc.vector.memset(tab_planes[:].bitcast(I32), 0)
        nc.vector.memset(w_planes[:].bitcast(I32), 0)
        nc.vector.memset(one[:], 1.0)
        nc.scalar.activation(warm[:], one[:], ACT.Abs_reciprocal_sqrt, bias=one[:])

        def load_vector(vec, name):
            sb = slot([P, BLOCKS, PACK], F32, name)
            nc.gpsimd.dma_start(out=sb[:], in_=vec.rearrange("(b p i) -> p b i", b=BLOCKS, i=PACK))
            return sb

        b1_sb = load_vector(b1, "b1_sb")
        base_sb = load_vector(base, "base_sb")
        rho_sb = load_vector(rho, "rho_sb")

        def load_planes(first, scales):
            for q in range(4):
                nc.sync.dma_start(
                    out=w_planes[32 * q + first : 32 * q + first + 4, :, :].bitcast(I32),
                    in_=scales[:, 4 * q : 4 * q + 4, :].bitcast(I32).rearrange("a r n -> r a n"),
                )

        make_identity(nc, ident[:])

        def load_rows(rows, name):
            raw = slot([P, PACK, BLOCK], F32, name)
            nc.sync.dma_start(out=raw[:], in_=rows.rearrange("(p j) c -> p j c", j=PACK))
            return raw

        def load_w1(b, a):
            return load_rows(w1[a * BLOCK : (a + 1) * BLOCK, b * BLOCK : (b + 1) * BLOCK], "raw%d%d" % (b, a))

        def load_table(a):
            words = slot([P, T], I32, "big%d" % a)
            nc.sync.dma_start(out=words[:], in_=tab_words[a].rearrange("p t i -> p (t i)").bitcast(I32))
            return words

        w1_raw = {}
        table = {}
        table[0] = load_table(0)
        for q in range(4):
            nc.sync.dma_start(
                out=tab_planes[32 * q : 32 * q + 4 * PASSES, :].bitcast(I32),
                in_=tab_scales[:, 4 * q : 4 * q + 4, :].bitcast(I32),
            )
        nc.sync.dma_start(offs_sb[:], offs)
        w1_raw[0, 0] = load_w1(0, 0)
        w1_raw[0, 1] = load_w1(0, 1)
        table[1] = load_table(1)
        table[2] = load_table(2)
        w1_raw[0, 2] = load_w1(0, 2)
        w1_raw[1, 0] = load_w1(1, 0)
        nc.sync.dma_start(offs2_sb[:], offs2)
        wgt_sb = keep.tile([P, M], F32, name="wgt_sb")
        nc.sync.dma_start(out=wgt_sb[:], in_=wgt)
        for a in range(1, PASSES):
            w1_raw[1, a] = load_w1(1, a)
        load_planes(4, wf_scales)
        w4_sb = keep.tile([P, BLOCKS, 2 * H], U8, name="w4_sb", align_bytes=64)
        nc.sync.dma_start(out=w4_sb[:].bitcast(I32), in_=w4_words.rearrange("a p c -> p a c").bitcast(I32))
        load_planes(0, w4_scales)
        wgo_sb = keep.tile([P, M], F32, name="wgo_sb")
        nc.sync.dma_start(out=wgo_sb[:], in_=wgo)
        nc.sync.dma_start(offs3_sb[:], offs3)

        pages = [keep.tile([P, T2], F32, name="page%d" % i) for i in range(BLOCKS * PACK)]
        for page in pages:
            nc.vector.memset(page[:], 0.0)

        def copy_on(engine, dst, src):
            if engine == "vector":
                nc.vector.tensor_copy(out=dst, in_=src)
            else:
                nc.scalar.copy(out=dst, in_=src)

        def quantise(grouped):
            codes = ring.tile([P, HALF], U32, name="codes", bufs=4, align_bytes=64)
            scales = ring.tile([P, HALF], U8, name="scales", bufs=4, align_bytes=64)
            nc.vector.quantize_mx(out=codes[:].bitcast(FP8X4), scales=scales[:], in_=grouped)
            return codes[:], scales[:]

        def quantise_pair(pair):
            codes = ring.tile([P, 2 * HALF], U32, name="codes2", bufs=6, align_bytes=64)
            scales = ring.tile([P, 2 * HALF], U8, name="scales2", bufs=6, align_bytes=64)
            nc.vector.quantize_mx(
                out=codes[:].bitcast(FP8X4), scales=scales[:], in_=pair[:].rearrange("p e n -> p (e n)")
            )
            return [(codes[:, e * HALF : (e + 1) * HALF], scales[:, e * HALF : (e + 1) * HALF]) for e in range(2)]

        def new_grouped():
            return ring.tile([P, HALF * PACK], BF16, name="grouped", bufs=2, align_bytes=64)[:]

        def round_w1(b, a, u, engine, grouped):
            src = w1_raw[b, a][:].rearrange("p j (m i) -> p m j i", i=PACK)[:, :, :, 2 * u : 2 * u + 2]
            copy_on(engine, grouped.rearrange("p (i m j) -> p m j i", i=2, j=PACK), src)

        w1_q = {}

        def pair_in(name):
            return slot([P, 2, HALF * PACK], BF16, name)

        def single_in(name):
            return slot([P, HALF * PACK], BF16, name)[:]

        def prepare_w1(b, units, engine, name):
            pair = pair_in(name)
            for e, (a, u) in enumerate(units):
                round_w1(b, a, u, engine, pair[:, e, :])
            for (a, u), q in zip(units, quantise_pair(pair)):
                w1_q[b, a, u] = q

        picked = {}

        def pick_words(a):
            picked[a] = keep.tile([P, S], U32, name="picked%d" % a, align_bytes=64)
            nc.vector.tensor_copy(out=picked[a][:], in_=table[a][:].bitcast(U32).indirect(offs_sb[:]))

        picked_planes = keep.tile([P, S], U8, name="picked_planes", align_bytes=64)

        def first_pass(b, a, banks, i):
            codes, scales = w1_q[b, a, i // 2]
            cols = slice((i % 2) * P, (i % 2 + 1) * P)
            for half in range(2):
                toks = slice(half * BANK, (half + 1) * BANK)
                nc.tensor.matmul_mx(
                    out=banks[2 * i + half][:],
                    lhsT=codes[:, cols].bitcast(FP8X4),
                    lhsT_scale=scales[:, cols],
                    rhs=picked[a][:, toks].bitcast(FP8X4),
                    rhs_scale=picked_planes[4 * a : P, toks],
                    start=(a == 0),
                    stop=(a == PASSES - 1),
                )

        x = {}

        def make_h(b, banks, i, name):
            h = slot([P, S], F32, name)
            bias = b1_sb[:, b, i : i + 1]
            for half in range(2):
                dst = h[:, half * BANK : (half + 1) * BANK]
                if (b, i, half) == (0, 0, 1):
                    nc.vector.tensor_scalar(dst, banks[2 * i + half][:], bias, None, ALU.add)
                else:
                    nc.scalar.activation(dst, banks[2 * i + half][:], ACT.Identity, bias=bias)
            return h

        def pick_x(b, i, h):
            whole = slot([P, M], F32, "x%d%d" % (b, i))
            nc.vector.tensor_tensor(whole[:], h[:].indirect(offs2_sb[:]), wgt_sb[:], ALU.mult)
            x[b, i] = whole[:]
            for half in range(2):
                x[b, i, half] = whole[:, half * HALF : (half + 1) * HALF]

        def pick_x_half(b, i, half, h, name):
            part = slot([P, HALF], F32, name)
            entries = offs2_sb[:, half * (HALF // 16) : (half + 1) * (HALF // 16)]
            nc.vector.tensor_tensor(
                part[:], h[:].indirect(entries), wgt_sb[:, half * HALF : (half + 1) * HALF], ALU.mult
            )
            x[b, i, half] = part[:]

        z_planes = {}

        def floor_x(b, i):
            nc.vector.tensor_scalar(z_planes[b][:, i, :], x[b, i], base_sb[:, b, i : i + 1], None, ALU.max)

        def floor_x_half(b, i, half):
            nc.vector.tensor_scalar(
                z_planes[b][:, i, half * HALF : (half + 1) * HALF], x[b, i, half],
                base_sb[:, b, i : i + 1], None, ALU.max,
            )

        def interleave(engine, planes, half, grouped):
            src = planes[:, :, half * HALF : (half + 1) * HALF].rearrange("p j (c e) -> p c j e", e=4)
            copy_on(engine, grouped.rearrange("p (c e j) -> p c j e", e=4, j=PACK), src)
            return grouped

        pick_words(0)
        nc.vector.tensor_copy(out=picked_planes[:], in_=tab_planes[:].indirect(offs_sb[:]))
        prepare_w1(0, [(0, 0), (0, 1)], "scalar", "h2")
        banks = [bank(k) for k in range(8)]
        for i in range(PACK):
            first_pass(0, 0, banks, i)
        prepare_w1(0, [(1, 0), (1, 1)], "scalar", "h3")
        pick_words(1)
        for i in range(PACK):
            first_pass(0, 1, banks, i)
        pick_words(2)
        foam_raw = [load_rows(foam[b * BLOCK : (b + 1) * BLOCK, :], "big%d" % b) for b in range(BLOCKS)]

        grouped = [single_in("big2"), new_grouped()]
        round_w1(0, 2, 0, "vector", grouped[0])
        round_w1(0, 2, 1, "scalar", grouped[1])
        for u in range(2):
            w1_q[0, 2, u] = quantise(grouped[u])
        h0 = []
        for i in range(PACK):
            first_pass(0, 2, banks, i)
            h0.append(make_h(0, banks, i, "h%d" % i))

        banks = [bank(k) for k in range(8)]
        prepare_w1(1, [(0, 0), (0, 1)], "vector", "big2")
        for i in range(PACK):
            pick_x(0, i, h0[i])
            first_pass(1, 0, banks, i)
        prepare_w1(1, [(1, 0), (2, 0)], "scalar", "big2")
        wf_sb = slot([P, BLOCKS, H], I32, "big2")
        nc.sync.dma_start(out=wf_sb[:], in_=wf_words.rearrange("a p c i -> p a (c i)").bitcast(I32))
        prepare_w1(1, [(1, 1), (2, 1)], "scalar", "h1")
        h1 = []
        for i in range(PACK):
            first_pass(1, 1, banks, i)
            first_pass(1, 2, banks, i)
            h1.append(make_h(1, banks, i, ("raw00", "raw01", "h2", "h3")[i]))
        z_planes[0] = slot([P, PACK, M], BF16, "h1")
        for i in range(PACK):
            floor_x(0, i)

        foam_q = {}
        z_q = {}

        def prepare_half(planes, half, name, quantised):
            pair = pair_in(name)
            for b in range(BLOCKS):
                interleave("scalar", planes[b], half, pair[:, b, :])
            for b, q in enumerate(quantise_pair(pair)):
                quantised[b, half] = q

        def wf_moving(b, nb):
            return wf_sb[:, b, nb * BLOCK : (nb + 1) * BLOCK].bitcast(FP8X4)

        def w4_moving(b, nb):
            return w4_sb[:, b, 2 * nb * BLOCK : 2 * (nb + 1) * BLOCK].bitcast(FP4X4)

        def second_pass(nb, half, b, c, acc, quantised, moving, first):
            codes, scales = quantised[b, half]
            cols = slice(c * P, (c + 1) * P)
            nc.tensor.matmul_mx(
                out=acc[:],
                lhsT=codes[:, cols].bitcast(FP8X4),
                lhsT_scale=scales[:, cols],
                rhs=moving(b, nb),
                rhs_scale=w_planes[first:P, b, nb * BLOCK : (nb + 1) * BLOCK],
                start=(b == 0),
                stop=(b == BLOCKS - 1),
            )

        def dealt(acc):
            return acc[:].rearrange("q (p i) -> q i p", i=PACK)

        phases = [(nb, half) for half in range(2) for nb in range(BLOCKS)]

        def damping(ph):
            nb, half = phases[ph]
            accs = [bank(c) for c in range(2)]
            for c in range(2):
                for b in range(BLOCKS):
                    second_pass(nb, half, b, c, accs[c], foam_q, wf_moving, 4)
            damp = [ring.tile([P, PACK, P], F32, name="damp", bufs=4) for c in range(2)]
            for c in range(2):
                nc.scalar.activation(damp[c][:], dealt(accs[c]), ACT.Abs)
            for c in range(2):
                root = slot([P, PACK, P], F32, "first_root" if (ph, c) == (0, 0) else "root%d" % c)
                nc.scalar.activation(root[:], damp[c][:], ACT.Abs_reciprocal_sqrt, bias=one[:])
                nc.scalar.activation(damp[c][:], root[:], ACT.Square)
            return damp

        def comfort_pass(ph, b, accs):
            nb, half = phases[ph]
            for c in range(2):
                second_pass(nb, half, b, c, accs[c], z_q, w4_moving, 0)

        def damp_comfort(acc, damp):
            nc.vector.tensor_tensor(damp[:], dealt(acc), damp[:], ALU.mult)

        def x_half(ph, i):
            nb, half = phases[ph]
            return x[nb, i, half]

        def turn_residual(ph):
            nb = phases[ph][0]
            accs = [bank(6 + c) for c in range(2)]
            for i in range(PACK):
                scaled = ring.tile([P, HALF], F32, name="scaled", bufs=4)
                nc.scalar.activation(scaled[:], x_half(ph, i), ACT.Copy, scale=rho_sb[:, nb, i : i + 1])
                for c in range(2):
                    nc.tensor.transpose(accs[c][:, i * P : (i + 1) * P], scaled[:, c * P : (c + 1) * P], ident[:])
            return accs

        def fetch_residual(ph, accs):
            turned = []
            for c in range(2):
                t = slot([P, PACK, P], F32, ("raw02", "raw10", "raw11", "raw12")[2 * (ph % 2) + c])
                nc.scalar.copy(out=t[:].rearrange("q i p -> q (i p)"), in_=accs[c][:])
                turned.append(t)
            return turned

        def make_y(ph, pair, damped, turned):
            nb = phases[ph][0]
            acc = bank(4 + pair)
            if pair == 1 and ph + 1 < len(phases):
                y = slot([P, 2, HALF], F32, "root1")
            else:
                y = ring.tile([P, 2, HALF], F32, name="y", bufs=2)
            for e in range(2):
                i = 2 * pair + e
                for c in range(2):
                    dst = acc[:, e * HALF + c * P : e * HALF + (c + 1) * P]
                    if turned is None:
                        nc.tensor.transpose(dst, damped[c][:, i, :], ident[:])
                    else:
                        nc.tensor.matmul(dst, damped[c][:, i, :], ident[:], start=True, stop=False, is_transpose=True)
                        nc.tensor.matmul(dst, turned[c][:, i, :], ident[:], start=False, stop=True, is_transpose=True)
            if turned is None:
                for e in range(2):
                    i = 2 * pair + e
                    nc.vector.scalar_tensor_tensor(
                        y[:, e, :], x_half(ph, i), rho_sb[:, nb, i : i + 1],
                        acc[:, e * HALF : (e + 1) * HALF], ALU.mult, ALU.add,
                    )
            else:
                nc.scalar.copy(out=y[:].rearrange("p e m -> p (e m)"), in_=acc[:])
            return y

        out_rows = out.rearrange("(b p i) t -> b i p t", b=BLOCKS, i=PACK)

        def file_y(ph, i, y):
            nb, half = phases[ph]
            page = pages[nb * PACK + i]
            places = offs3_sb[:, half * (HALF // 16) : (half + 1) * (HALF // 16)]
            nc.vector.tensor_tensor(
                page[:].indirect(places), y, wgo_sb[:, half * HALF : (half + 1) * HALF], ALU.mult
            )
            if half == 1:
                nc.sync.dma_start(out=out_rows[nb, i], in_=page[:])

        pick_x(1, 0, h1[0])
        grouped = interleave("vector", z_planes[0], 0, new_grouped())
        pick_x(1, 1, h1[1])
        z_q[0, 0] = quantise(grouped)
        accs = [bank(2 + c) for c in range(2)]
        comfort_pass(0, 0, accs)
        prepare_half(foam_raw, 0, "b1_sb", foam_q)
        z_planes[1] = slot([P, PACK, M], BF16, "h0")
        floor_x(1, 0)
        floor_x(1, 1)
        pick_x_half(1, 2, 0, h1[2], "b1_sb")
        pick_x_half(1, 3, 0, h1[3], "x130")
        damp = damping(0)
        floor_x_half(1, 2, 0)
        floor_x_half(1, 3, 0)
        z_q[1, 0] = quantise(interleave("vector", z_planes[1], 0, single_in("raw00")))
        comfort_pass(0, 1, accs)
        pick_x_half(1, 2, 1, h1[2], "raw00")
        damp_comfort(accs[0], damp[0])
        pick_x_half(1, 3, 1, h1[3], "first_root")
        damp_comfort(accs[1], damp[1])
        floor_x_half(1, 2, 1)
        floor_x_half(1, 3, 1)

        turned = None
        y = make_y(0, 0, damp, turned)
        for ph in range(len(phases) - 1):
            file_y(ph, 0, y[:, 0, :])
            residual = turn_residual(ph + 1)
            next_damp = damping(ph + 1)
            accs = [bank(2 + c) for c in range(2)]
            for b in range(BLOCKS):
                comfort_pass(ph + 1, b, accs)
            file_y(ph, 1, y[:, 1, :])
            for c in range(2):
                damp_comfort(accs[c], next_damp[c])
            y = make_y(ph, 1, damp, turned)
            turned = fetch_residual(ph + 1, residual)
            file_y(ph, 2, y[:, 0, :])
            file_y(ph, 3, y[:, 1, :])
            if ph == 0:
                prepare_half(foam_raw, 1, "raw01", foam_q)
                prepare_half(z_planes, 1, "h3", z_q)
            damp = next_damp
            y = make_y(ph + 1, 0, damp, turned)
        last = len(phases) - 1
        y_rest = make_y(last, 1, damp, turned)
        for i in range(PACK):
            file_y(last, i, (y, y_rest)[i // 2][:, i % 2, :])
